import numpy as np
import ml_dtypes


def mxq(x, axis, fmt="e4m3"):
    dtype, down = {"e4m3": (ml_dtypes.float8_e4m3fn, 7), "e5m2": (ml_dtypes.float8_e5m2, 14)}[fmt]
    v = np.moveaxis(np.asarray(x, np.float32).astype(ml_dtypes.bfloat16).astype(np.float64), axis, -1)
    blocks = v.reshape(v.shape[:-1] + (-1, 32))
    amax = np.abs(blocks).max(-1, keepdims=True)
    byte = np.maximum(np.where(amax > 0, np.frexp(amax)[1] - 1 + 127, 0) - down, 1)
    scale = np.exp2(byte - 127.0)
    codes = (blocks / scale).astype(np.float32).astype(dtype).astype(np.float64)
    return np.moveaxis((codes * scale).reshape(v.shape), -1, axis)


WIDE = False


def mx_kscale(k):
    if not WIDE:
        return np.ones(k)
    levels = np.array([10, -10, 5, -5, 0])
    if k % 512:
        return np.exp2(np.random.permutation(np.resize(levels, k // 32))).repeat(32)
    a = np.empty((k // 512, 16))
    for p in range(k // 512):
        a[p, :8] = np.random.permutation(np.resize(levels, 8))
        for g in range(8):
            far = levels[np.abs(levels - a[p, g]) >= 10]
            a[p, g + 8] = far[np.random.randint(len(far))]
    return np.exp2(a.ravel()).repeat(32)


def f64(x):
    return np.asarray(x).astype(np.float64)


def striped(idx):
    return np.tile(idx.reshape(-1, 16).T, (8, 1)).astype(np.uint16)


def unstriped(offs):
    return offs[:16].T.reshape(-1).astype(np.int64)


E2M1 = np.array([0.0, 0.5, 1.0, 1.5, 2.0, 3.0, 4.0, 6.0, -0.0, -0.5, -1.0, -1.5, -2.0, -3.0, -4.0, -6.0])


def pack_weight(w, fmt):
    k, n = w.shape
    w = f64(np.asarray(w, np.float32).astype(ml_dtypes.bfloat16)).reshape(k // 32, 32, n)
    amax = np.abs(w).max(1)
    if fmt == "e4m3":
        byte = np.frexp(amax)[1] - 1 + 127 - 7
    else:
        mant, ex = np.frexp(amax / 6.0)
        byte = np.where(mant > 0.5, ex, ex - 1) + 127
    byte = np.clip(np.where(amax > 0, byte, 1), 1, 254)
    scaled = (w * np.exp2(127.0 - byte)[:, None, :]).reshape(k, n).astype(np.float32)
    by_word = np.ascontiguousarray(scaled.reshape(k // 512, 128, 4, n).transpose(0, 1, 3, 2))
    if fmt == "e4m3":
        words = by_word.astype(ml_dtypes.float8_e4m3fn).view(np.uint8)
    else:
        c = by_word.astype(ml_dtypes.float4_e2m1fn).view(np.uint8) & 0xF
        words = (c[..., 0::2] | (c[..., 1::2] << 4)).reshape(k // 512, 128, 2 * n)
    return np.ascontiguousarray(words), np.ascontiguousarray(byte.astype(np.uint8).reshape(k // 512, 16, n))


def unpack_weight(words, scales, fmt):
    g, _, n = scales.shape
    words = np.ascontiguousarray(words).reshape(g, 128, n, -1)
    if fmt == "e4m3":
        vals = words.view(ml_dtypes.float8_e4m3fn).astype(np.float64)
    else:
        nib = np.empty((g, 128, n, 4), np.uint8)
        nib[..., 0::2] = words & 0xF
        nib[..., 1::2] = words >> 4
        vals = E2M1[nib]
    vals = vals * np.repeat(np.exp2(scales.astype(np.float64) - 127.0), 8, axis=1)[..., None]
    return vals.transpose(0, 1, 3, 2).reshape(g * 512, n)


def gelu(v):
    return 0.5 * v * (1.0 + np.tanh(np.sqrt(2.0 / np.pi) * (v + 0.044715 * v**3)))


K, T, S, H, S2, T3, T2 = 1536, 4096, 1024, 512, 512, 2048, 2048


def setup_inputs():
    n = np.random.standard_normal
    s = mx_kscale(K)[:, None]
    u = mx_kscale(H)[:, None]
    tab_words, tab_scales = pack_weight(n((K, T)) * s, "e4m3")
    tab2_words, tab2_scales = pack_weight(n((H, T3)) / np.sqrt(H) / u, "e4m3")
    w1_words, w1_scales = pack_weight(1.2 * n((K, H)) / np.sqrt(K) / s, "e2m1")
    return {
        "tab_words": tab_words, "tab_scales": tab_scales,
        "offs": striped(np.random.permutation(T)[:S]),
        "tab2_words": tab2_words, "tab2_scales": tab2_scales,
        "offs2": striped(np.random.permutation(T3)[:S2]),
        "offs3": striped(np.random.permutation(T2)[:S]),
        "w1_words": w1_words, "w1_scales": w1_scales,
        "b1": (0.7 * n(H)).astype(np.float32),
        "clock": (1.5 * n((H, S)) * u).astype(np.float32),
        "wd": (1.3 * n((K, S2)) / np.sqrt(K) / s).astype(np.float32),
        "gs": np.exp(0.4 * n(S2)).astype(np.float32),
        "wgo": np.exp(0.3 * n((128, S))).astype(np.float32),
        "page1": n((S2, T2)).astype(np.float32),
    }


def reference(tab_words, tab_scales, offs, tab2_words, tab2_scales, offs2, offs3,
              w1_words, w1_scales, b1, clock, wd, gs, wgo, page1):
    v = unpack_weight(tab_words, tab_scales, "e4m3")[:, unstriped(offs)]
    v2 = unpack_weight(tab2_words, tab2_scales, "e4m3")[:, unstriped(offs2)]
    w1 = unpack_weight(w1_words, w1_scales, "e2m1")
    h = np.tanh((w1.T @ v) + f64(b1)[:, None]) * f64(clock)
    e = v2.T @ mxq(h, 0, "e4m3")
    d = mxq(f64(wd), 0, "e4m3").T @ v
    y = (np.maximum(e, d) + np.tanh(d)) * f64(gs)[:, None]
    out = f64(page1).copy()
    out[:, unstriped(offs3)] = np.tile(f64(wgo), (S2 // 128, 1)) * y
    return out

@@ -1,0 +1,297 @@
+from contextlib import ExitStack
+
+import concourse.mybir as mybir
+from concourse.masks import make_identity
+
+K, T, S, H, S2, T3, T2 = 1536, 4096, 1024, 512, 512, 2048, 2048
+FLOPS = 2 * (K * H * S + H * S2 * S + K * S2 * S)
+
+F32 = mybir.dt.float32
+BF16 = mybir.dt.bfloat16
+I32 = mybir.dt.int32
+U32 = mybir.dt.uint32
+U16 = mybir.dt.uint16
+U8 = mybir.dt.uint8
+FP8X4 = mybir.dt.float8_e4m3fn_x4
+FP4X4 = mybir.dt.float4_e2m1fn_x4
+ACT = mybir.ActivationFunctionType
+ALU = mybir.AluOpType
+
+P = 128
+PACK = 4
+K_PASS = P * PACK
+PASSES = K // K_PASS
+BANK = 512
+QUARTER = S // 4
+HALF = S // 2
+M_HALF = S2 // 2
+STRIPE = 16
+PARKED = (4, 68)
+
+CHUNKS = [(q * QUARTER, QUARTER, 0, M_HALF) for q in range(4)] + [
+    (h * HALF, HALF, mt * P, P) for mt in (2, 3) for h in range(2)
+]
+
+
+def tile_list_promotion_page_scores_kernel(
+    tc, tab_words, tab_scales, offs, tab2_words, tab2_scales, offs2, offs3,
+    w1_words, w1_scales, b1, clock, wd, gs, wgo, page1, out,
+):
+    nc = tc.nc
+    with ExitStack() as ctx:
+        keep = ctx.enter_context(tc.tile_pool(name="keep", bufs=1))
+        ring = ctx.enter_context(tc.tile_pool(name="ring", bufs=2))
+        psum = ctx.enter_context(tc.psum_pool(name="psum", bufs=1))
+
+        def held(shape, dtype, name):
+            return keep.tile(shape, dtype, name=name, align_bytes=64)
+
+        idx = held([P, S // STRIPE], U16, "idx")
+        idx2 = held([P, S2 // STRIPE], U16, "idx2")
+        idx3 = held([P, S // STRIPE], U16, "idx3")
+        tab_w = [held([P, T], I32, "tab_w%d" % a) for a in range(PASSES)]
+        tab_s = held([P, T], U8, "tab_s")
+        tab2_w = held([P, T3], I32, "tab2_w")
+        tab2_s = held([P, T3], U8, "tab2_s")
+        w1_raw = held([P, PASSES * 2 * H], U8, "w1_raw")
+        w1_raw_s = held([P, PASSES * H], U8, "w1_raw_s")
+        w1_w = held([P, PASSES * 2 * H], U8, "w1_w")
+        w1_s = held([P, PASSES * H], U8, "w1_s")
+        v_w = [held([P, S], U32, "v_w%d" % a) for a in range(PASSES)]
+        v_s0 = held([P, S], U8, "v_s0")
+        v_s12 = held([P, (PASSES - 1) * S], U8, "v_s12")
+        v2_w = held([P, S2], U32, "v2_w")
+        v2_s = held([P, S2], U8, "v2_s")
+        b1_sb = held([P, PACK], F32, "b1_sb")
+        gs_sb = held([P, S2 // P], F32, "gs_sb")
+        clock_sb = [held([P, PACK, QUARTER], F32, "clock%d" % q) for q in range(4)]
+        wd_raw = {(a, g): held([P, PACK, M_HALF], F32, "wd_raw%d%d" % (a, g)) for g in range(2) for a in range(PASSES)}
+        wd_w = {(a, g): held([P, M_HALF], U32, "wd_w%d%d" % (a, g)) for g in range(2) for a in range(PASSES)}
+        wd_s = {(a, g): held([P, M_HALF], U8, "wd_s%d%d" % (a, g)) for g in range(2) for a in range(PASSES)}
+        h_w = [held([P, QUARTER], U32, "h_w%d" % q) for q in range(4)]
+        h_s = [held([P, QUARTER], U8, "h_s%d" % q) for q in range(4)]
+        wgo_sb = held([P, S], F32, "wgo_sb")
+        page = [held([P, T2], F32, "page%d" % mt) for mt in range(S2 // P)]
+        ident = held([P, P], F32, "ident")
+
+        x_bank = [psum.tile([P, BANK], F32, name="x_bank%d" % i) for i in range(2)]
+        e_bank = [psum.tile([P, BANK], F32, name="e_bank%d" % i) for i in range(2)]
+        d_bank = [psum.tile([P, BANK], F32, name="d_bank%d" % i) for i in range(2)]
+        y_bank = [psum.tile([P, BANK], F32, name="y_bank%d" % i) for i in range(2)]
+
+        def v_scales(a, cols):
+            if a == 0:
+                return v_s0[:, cols]
+            return v_s12[:, (a - 1) * S + cols.start : (a - 1) * S + cols.stop]
+
+        for tile in (tab_s, w1_raw_s, v_s12, tab2_s):
+            nc.vector.memset(tile[:].bitcast(I32), 0)
+
+        def load_words(tile, words):
+            nc.sync.dma_start(tile[:], words.rearrange("p n t -> p (n t)").bitcast(I32))
+
+        def load_clock(q):
+            nc.sync.dma_start(
+                clock_sb[q][:], clock[:, q * QUARTER : (q + 1) * QUARTER].rearrange("(p t) j -> p t j", t=PACK)
+            )
+
+        def load_wd(g, passes):
+            for a in passes:
+                rows = wd[a * K_PASS : (a + 1) * K_PASS, g * M_HALF : (g + 1) * M_HALF]
+                nc.sync.dma_start(wd_raw[a, g][:], rows.rearrange("(p t) m -> p t m", t=PACK))
+
+        def load_page(mt):
+            nc.sync.dma_start(page[mt][:], page1[mt * P : (mt + 1) * P, :])
+
+        def load_wgo(q):
+            cols = slice(q * QUARTER, (q + 1) * QUARTER)
+            nc.sync.dma_start(wgo_sb[:, cols], wgo[:, cols])
+
+        nc.sync.dma_start(idx[:], offs)
+        load_words(tab_w[0], tab_words[0])
+        for a in range(1, PASSES):
+            first = PARKED[a - 1]
+            nc.scalar.dma_start(tab_s[first : first + 16, :].bitcast(I32), tab_scales[a].bitcast(I32))
+        for q in range(4):
+            nc.scalar.dma_start(
+                tab_s[32 * q : 32 * q + 4, :].bitcast(I32), tab_scales[0, 4 * q : 4 * q + 4, :].bitcast(I32)
+            )
+        nc.sync.dma_start(
+            w1_raw[:].bitcast(I32).rearrange("p (a n) -> p a n", a=PASSES),
+            w1_words.bitcast(I32).rearrange("a p n -> p a n"),
+        )
+        for q in range(4):
+            nc.sync.dma_start(
+                w1_raw_s[32 * q : 32 * q + 4, :].bitcast(I32).rearrange("r (a n) -> r a n", a=PASSES),
+                w1_scales[:, 4 * q : 4 * q + 4, :].bitcast(I32).rearrange("a r n -> r a n"),
+            )
+        load_words(tab_w[1], tab_words[1])
+        nc.sync.dma_start(idx2[:], offs2)
+        for q in range(4):
+            nc.sync.dma_start(
+                tab2_s[32 * q : 32 * q + 4, :].bitcast(I32), tab2_scales[0, 4 * q : 4 * q + 4, :].bitcast(I32)
+            )
+        nc.sync.dma_start(b1_sb[:], b1.rearrange("(p t) -> p t", t=PACK))
+        load_words(tab_w[2], tab_words[2])
+        load_wd(0, range(PASSES))
+        load_words(tab2_w, tab2_words[0])
+        load_clock(0)
+        load_clock(1)
+        with nc.allow_non_contiguous_dma(reason="one gain for each partition"):
+            nc.sync.dma_start(gs_sb[:], gs.rearrange("(mt p) -> p mt", p=P))
+        nc.sync.dma_start(idx3[:], offs3)
+        load_wgo(0)
+        load_page(0)
+        load_page(1)
+        load_clock(2)
+        load_clock(3)
+        load_wd(1, range(0, 1))
+        load_wgo(1)
+        load_wd(1, range(1, PASSES))
+        load_page(2)
+        load_wgo(2)
+        load_page(3)
+        load_wgo(3)
+
+        make_identity(nc, ident[:])
+
+        nc.vector.tensor_copy(v_s0[:], tab_s[:].indirect(idx[:]))
+        for a in range(1, PASSES):
+            for q in range(4):
+                first = PARKED[a - 1] + 4 * q
+                nc.gpsimd.dma_start(
+                    v_s12[32 * q : 32 * q + 4, (a - 1) * S : a * S].bitcast(I32),
+                    v_s0[first : first + 4, :].bitcast(I32),
+                )
+        nc.vector.tensor_copy(
+            w1_w[:].bitcast(U16).rearrange("p (a t m) -> p a t m", a=PASSES, t=PACK),
+            w1_raw[:].bitcast(U16).rearrange("p (a m t) -> p a t m", a=PASSES, t=PACK),
+        )
+        nc.vector.tensor_copy(
+            w1_s[:].rearrange("p (a t m) -> p a t m", a=PASSES, t=PACK),
+            w1_raw_s[:].rearrange("p (a m t) -> p a t m", a=PASSES, t=PACK),
+        )
+        for a in range(PASSES - 1):
+            nc.vector.tensor_copy(v_w[a][:], tab_w[a][:].bitcast(U32).indirect(idx[:]))
+        nc.vector.tensor_copy(v2_s[:], tab2_s[:].indirect(idx2[:]))
+        for h in range(2):
+            nc.vector.tensor_copy(
+                v_w[PASSES - 1][:, h * HALF : (h + 1) * HALF],
+                tab_w[PASSES - 1][:].bitcast(U32).indirect(idx[:, h * HALF // STRIPE : (h + 1) * HALF // STRIPE]),
+            )
+
+        def features(q):
+            cols = slice(q * QUARTER, (q + 1) * QUARTER)
+            for a in range(PASSES):
+                for t in range(PACK):
+                    c0 = a * H + t * P
+                    nc.tensor.matmul_mx(
+                        out=x_bank[t // 2][:, (t % 2) * QUARTER : (t % 2 + 1) * QUARTER],
+                        lhsT=w1_w[:, 2 * c0 : 2 * (c0 + P)].bitcast(FP4X4),
+                        lhsT_scale=w1_s[:, c0 : c0 + P],
+                        rhs=v_w[a][:, cols].bitcast(FP8X4),
+                        rhs_scale=v_scales(a, cols),
+                        start=(a == 0 and t % 2 == 0),
+                        stop=(a == PASSES - 1 and t % 2 == 1),
+                    )
+            feat = ring.tile([P, PACK, QUARTER], F32, name="feat")
+            for t in range(PACK):
+                nc.scalar.activation(
+                    feat[:, t, :], x_bank[t // 2][:, (t % 2) * QUARTER : (t % 2 + 1) * QUARTER],
+                    ACT.Tanh, bias=b1_sb[:, t : t + 1],
+                )
+            h_bf = ring.tile([P, QUARTER, PACK], BF16, name="h_bf", align_bytes=64)
+            nc.vector.tensor_tensor(
+                h_bf[:].rearrange("p (c i) t -> p c t i", i=4),
+                feat[:].rearrange("p t (c i) -> p c t i", i=4),
+                clock_sb[q][:].rearrange("p t (c i) -> p c t i", i=4),
+                ALU.mult,
+            )
+            nc.vector.quantize_mx(
+                out=h_w[q][:].bitcast(FP8X4), scales=h_s[q][:], in_=h_bf[:].rearrange("p j t -> p (j t)")
+            )
+
+        def styles():
+            nc.vector.tensor_copy(v2_w[:], tab2_w[:].bitcast(U32).indirect(idx2[:]))
+
+        def direct_weights(g):
+            for a in range(PASSES):
+                wd_bf = ring.tile([P, M_HALF, PACK], BF16, name="wd_bf", align_bytes=64, bufs=3)
+                nc.scalar.copy(
+                    wd_bf[:].rearrange("p (c i) t -> p c t i", i=4),
+                    wd_raw[a, g][:].rearrange("p t (c i) -> p c t i", i=4),
+                )
+                nc.vector.quantize_mx(
+                    out=wd_w[a, g][:].bitcast(FP8X4), scales=wd_s[a, g][:],
+                    in_=wd_bf[:].rearrange("p m t -> p (m t)"),
+                )
+
+        def scores(c):
+            j0, jn, m0, mn = CHUNKS[c]
+            blocks = jn // P
+            g, mc = divmod(m0, M_HALF)
+            e_ps, d_ps, y_ps = e_bank[c % 2], d_bank[c % 2], y_bank[c % 2]
+            for a in range(PASSES):
+                for b in range(blocks):
+                    cols = slice(j0 + b * P, j0 + (b + 1) * P)
+                    nc.tensor.matmul_mx(
+                        out=d_ps[:, b * mn : (b + 1) * mn],
+                        lhsT=v_w[a][:, cols].bitcast(FP8X4),
+                        lhsT_scale=v_scales(a, cols),
+                        rhs=wd_w[a, g][:, mc : mc + mn].bitcast(FP8X4),
+                        rhs_scale=wd_s[a, g][:, mc : mc + mn],
+                        start=(a == 0 and b == 0),
+                        stop=(a == PASSES - 1 and b == blocks - 1),
+                    )
+            for b in range(blocks):
+                q, jc = divmod(j0 + b * P, QUARTER)
+                nc.tensor.matmul_mx(
+                    out=e_ps[:, b * mn : (b + 1) * mn],
+                    lhsT=h_w[q][:, jc : jc + P].bitcast(FP8X4),
+                    lhsT_scale=h_s[q][:, jc : jc + P],
+                    rhs=v2_w[:, m0 : m0 + mn].bitcast(FP8X4),
+                    rhs_scale=v2_s[:, m0 : m0 + mn],
+                    start=True,
+                    stop=True,
+                )
+            d_sb = ring.tile([P, BANK], F32, name="d_sb")
+            nc.scalar.copy(d_sb[:], d_ps[:])
+            tanh_d = ring.tile([P, BANK], F32, name="tanh_d")
+            nc.scalar.activation(tanh_d[:], d_ps[:], ACT.Tanh)
+            top = ring.tile([P, BANK], F32, name="top")
+            nc.vector.tensor_tensor(top[:], e_ps[:], d_sb[:], ALU.max)
+            for u in range(mn // P):
+                for b in range(blocks):
+                    src = slice(b * mn + u * P, b * mn + (u + 1) * P)
+                    dst = y_ps[:, u * jn + b * P : u * jn + (b + 1) * P]
+                    nc.tensor.matmul(dst, tanh_d[:, src], ident[:], start=True, stop=False, is_transpose=True)
+                    nc.tensor.matmul(dst, top[:, src], ident[:], start=False, stop=True, is_transpose=True)
+
+        def place(c):
+            j0, jn, m0, mn = CHUNKS[c]
+            for u in range(mn // P):
+                mt = m0 // P + u
+                y_sb = ring.tile([P, jn], F32, name="y_sb", bufs=4)
+                nc.scalar.activation(
+                    y_sb[:], y_bank[c % 2][:, u * jn : (u + 1) * jn], ACT.Copy, scale=gs_sb[:, mt : mt + 1]
+                )
+                nc.vector.tensor_tensor(
+                    page[mt][:].indirect(idx3[:, j0 // STRIPE : (j0 + jn) // STRIPE]),
+                    y_sb[:], wgo_sb[:, j0 : j0 + jn], ALU.mult,
+                )
+                if j0 + jn == S:
+                    nc.sync.dma_start(out[mt * P : (mt + 1) * P, :], page[mt][:])
+
+        direct_weights(0)
+        styles()
+        features(0)
+        features(1)
+        scores(0)
+        for c in range(1, len(CHUNKS)):
+            if c + 1 < 4:
+                features(c + 1)
+            if c == 3:
+                direct_weights(1)
+            scores(c)
+            place(c - 1)
+        place(len(CHUNKS) - 1)

@@ -72,12 +72,18 @@ def tile_list_promotion_page_scores_kernel(
         h_s = [held([P, QUARTER], U8, "h_s%d" % q) for q in range(4)]
         wgo_sb = held([P, S], F32, "wgo_sb")
         page = [held([P, T2], F32, "page%d" % mt) for mt in range(S2 // P)]
+        stage = [held([P, BANK], F32, "stage%d" % i) for i in range(6)]
         ident = held([P, P], F32, "ident")
 
         x_bank = [psum.tile([P, BANK], F32, name="x_bank%d" % i) for i in range(2)]
         e_bank = [psum.tile([P, BANK], F32, name="e_bank%d" % i) for i in range(2)]
         d_bank = [psum.tile([P, BANK], F32, name="d_bank%d" % i) for i in range(2)]
         y_bank = [psum.tile([P, BANK], F32, name="y_bank%d" % i) for i in range(2)]
+
+        score_banks = [(e_bank[0], d_bank[0]), (e_bank[1], d_bank[1]), (x_bank[0], x_bank[1])]
+        feature_banks = [x_bank, score_banks[1], y_bank, x_bank]
+        terms = {}
+        feats = {}
 
         def v_scales(a, cols):
             if a == 0:
@@ -88,7 +94,19 @@ def tile_list_promotion_page_scores_kernel(
             nc.vector.memset(tile[:].bitcast(I32), 0)
 
         def load_words(tile, words):
-            nc.sync.dma_start(tile[:], words.rearrange("p n t -> p (n t)").bitcast(I32))
+            nc.sync.dma_start(tile, words.rearrange("p n t -> p (n t)").bitcast(I32))
+
+        def load_tab(a, h):
+            cols = slice(h * T // 2, (h + 1) * T // 2)
+            load_words(tab_w[a][:, cols], tab_words[a, :, cols, :])
+
+        def move_scales(a):
+            for q in range(4):
+                first = PARKED[a - 1] + 4 * q
+                nc.sync.dma_start(
+                    v_s12[32 * q : 32 * q + 4, (a - 1) * S : a * S].bitcast(I32),
+                    v_s0[first : first + 4, :].bitcast(I32),
+                )
 
         def load_clock(q):
             nc.sync.dma_start(
@@ -108,34 +126,42 @@ def tile_list_promotion_page_scores_kernel(
             nc.sync.dma_start(wgo_sb[:, cols], wgo[:, cols])
 
         nc.sync.dma_start(idx[:], offs)
-        load_words(tab_w[0], tab_words[0])
-        for a in range(1, PASSES):
-            first = PARKED[a - 1]
-            nc.scalar.dma_start(tab_s[first : first + 16, :].bitcast(I32), tab_scales[a].bitcast(I32))
-        for q in range(4):
-            nc.scalar.dma_start(
-                tab_s[32 * q : 32 * q + 4, :].bitcast(I32), tab_scales[0, 4 * q : 4 * q + 4, :].bitcast(I32)
-            )
         nc.sync.dma_start(
             w1_raw[:].bitcast(I32).rearrange("p (a n) -> p a n", a=PASSES),
             w1_words.bitcast(I32).rearrange("a p n -> p a n"),
         )
+        load_tab(0, 0)
+        for a in range(1, PASSES):
+            first = PARKED[a - 1]
+            nc.sync.dma_start(tab_s[first : first + 16, :].bitcast(I32), tab_scales[a].bitcast(I32))
+        for q in range(4):
+            nc.sync.dma_start(
+                tab_s[32 * q : 32 * q + 4, :].bitcast(I32), tab_scales[0, 4 * q : 4 * q + 4, :].bitcast(I32)
+            )
+        load_tab(0, 1)
         for q in range(4):
             nc.sync.dma_start(
                 w1_raw_s[32 * q : 32 * q + 4, :].bitcast(I32).rearrange("r (a n) -> r a n", a=PASSES),
                 w1_scales[:, 4 * q : 4 * q + 4, :].bitcast(I32).rearrange("a r n -> r a n"),
             )
-        load_words(tab_w[1], tab_words[1])
+        load_tab(1, 0)
+        nc.vector.tensor_copy(v_s0[:], tab_s[:].indirect(idx[:]))
+        move_scales(1)
+        load_tab(1, 1)
+        move_scales(2)
+        load_tab(2, 0)
         nc.sync.dma_start(idx2[:], offs2)
         for q in range(4):
             nc.sync.dma_start(
                 tab2_s[32 * q : 32 * q + 4, :].bitcast(I32), tab2_scales[0, 4 * q : 4 * q + 4, :].bitcast(I32)
             )
+        load_tab(2, 1)
         nc.sync.dma_start(b1_sb[:], b1.rearrange("(p t) -> p t", t=PACK))
-        load_words(tab_w[2], tab_words[2])
         load_wd(0, range(PASSES))
-        load_words(tab2_w, tab2_words[0])
         load_clock(0)
+        for h in range(2):
+            cols = slice(h * T3 // 2, (h + 1) * T3 // 2)
+            load_words(tab2_w[:, cols], tab2_words[0, :, cols, :])
         load_clock(1)
         with nc.allow_non_contiguous_dma(reason="one gain for each partition"):
             nc.sync.dma_start(gs_sb[:], gs.rearrange("(mt p) -> p mt", p=P))
@@ -155,21 +181,13 @@ def tile_list_promotion_page_scores_kernel(
 
         make_identity(nc, ident[:])
 
-        nc.vector.tensor_copy(v_s0[:], tab_s[:].indirect(idx[:]))
-        for a in range(1, PASSES):
-            for q in range(4):
-                first = PARKED[a - 1] + 4 * q
-                nc.gpsimd.dma_start(
-                    v_s12[32 * q : 32 * q + 4, (a - 1) * S : a * S].bitcast(I32),
-                    v_s0[first : first + 4, :].bitcast(I32),
-                )
         nc.vector.tensor_copy(
-            w1_w[:].bitcast(U16).rearrange("p (a t m) -> p a t m", a=PASSES, t=PACK),
-            w1_raw[:].bitcast(U16).rearrange("p (a m t) -> p a t m", a=PASSES, t=PACK),
+            w1_w[:].bitcast(U16).rearrange("p (a t c i) -> p a c t i", a=PASSES, t=PACK, i=8),
+            w1_raw[:].bitcast(U16).rearrange("p (a c i t) -> p a c t i", a=PASSES, t=PACK, i=8),
         )
         nc.vector.tensor_copy(
-            w1_s[:].rearrange("p (a t m) -> p a t m", a=PASSES, t=PACK),
-            w1_raw_s[:].rearrange("p (a m t) -> p a t m", a=PASSES, t=PACK),
+            w1_s[:].rearrange("p (a t c i) -> p a c t i", a=PASSES, t=PACK, i=16),
+            w1_raw_s[:].rearrange("p (a c i t) -> p a c t i", a=PASSES, t=PACK, i=16),
         )
         for a in range(PASSES - 1):
             nc.vector.tensor_copy(v_w[a][:], tab_w[a][:].bitcast(U32).indirect(idx[:]))
@@ -186,7 +204,7 @@ def tile_list_promotion_page_scores_kernel(
                 for t in range(PACK):
                     c0 = a * H + t * P
                     nc.tensor.matmul_mx(
-                        out=x_bank[t // 2][:, (t % 2) * QUARTER : (t % 2 + 1) * QUARTER],
+                        out=feature_banks[q][t // 2][:, (t % 2) * QUARTER : (t % 2 + 1) * QUARTER],
                         lhsT=w1_w[:, 2 * c0 : 2 * (c0 + P)].bitcast(FP4X4),
                         lhsT_scale=w1_s[:, c0 : c0 + P],
                         rhs=v_w[a][:, cols].bitcast(FP8X4),
@@ -194,21 +212,25 @@ def tile_list_promotion_page_scores_kernel(
                         start=(a == 0 and t % 2 == 0),
                         stop=(a == PASSES - 1 and t % 2 == 1),
                     )
-            feat = ring.tile([P, PACK, QUARTER], F32, name="feat")
+            feat = ring.tile([P, PACK, QUARTER], F32, name="feat", bufs=4)
             for t in range(PACK):
                 nc.scalar.activation(
-                    feat[:, t, :], x_bank[t // 2][:, (t % 2) * QUARTER : (t % 2 + 1) * QUARTER],
+                    feat[:, t, :], feature_banks[q][t // 2][:, (t % 2) * QUARTER : (t % 2 + 1) * QUARTER],
                     ACT.Tanh, bias=b1_sb[:, t : t + 1],
                 )
-            h_bf = ring.tile([P, QUARTER, PACK], BF16, name="h_bf", align_bytes=64)
+            feats[q] = feat
+
+        def quantise_features(q):
+            feat = feats[q]
+            h_bf = stage[(q + 4) % 6][:].bitcast(BF16)
             nc.vector.tensor_tensor(
-                h_bf[:].rearrange("p (c i) t -> p c t i", i=4),
+                h_bf.rearrange("p (c i t) -> p c t i", i=4, t=PACK),
                 feat[:].rearrange("p t (c i) -> p c t i", i=4),
                 clock_sb[q][:].rearrange("p t (c i) -> p c t i", i=4),
                 ALU.mult,
             )
             nc.vector.quantize_mx(
-                out=h_w[q][:].bitcast(FP8X4), scales=h_s[q][:], in_=h_bf[:].rearrange("p j t -> p (j t)")
+                out=h_w[q][:].bitcast(FP8X4), scales=h_s[q][:], in_=h_bf
             )
 
         def styles():
@@ -216,21 +238,22 @@ def tile_list_promotion_page_scores_kernel(
 
         def direct_weights(g):
             for a in range(PASSES):
-                wd_bf = ring.tile([P, M_HALF, PACK], BF16, name="wd_bf", align_bytes=64, bufs=3)
-                nc.scalar.copy(
-                    wd_bf[:].rearrange("p (c i) t -> p c t i", i=4),
+                wd_bf = stage[a][:].bitcast(BF16)
+                cast = nc.vector.tensor_copy if g == 0 and a < PASSES - 1 else nc.scalar.copy
+                cast(
+                    wd_bf.rearrange("p (c i t) -> p c t i", i=4, t=PACK),
                     wd_raw[a, g][:].rearrange("p t (c i) -> p c t i", i=4),
                 )
                 nc.vector.quantize_mx(
                     out=wd_w[a, g][:].bitcast(FP8X4), scales=wd_s[a, g][:],
-                    in_=wd_bf[:].rearrange("p m t -> p (m t)"),
+                    in_=wd_bf,
                 )
 
         def scores(c):
             j0, jn, m0, mn = CHUNKS[c]
             blocks = jn // P
             g, mc = divmod(m0, M_HALF)
-            e_ps, d_ps, y_ps = e_bank[c % 2], d_bank[c % 2], y_bank[c % 2]
+            e_ps, d_ps = score_banks[c % 3]
             for a in range(PASSES):
                 for b in range(blocks):
                     cols = slice(j0 + b * P, j0 + (b + 1) * P)
@@ -254,12 +277,19 @@ def tile_list_promotion_page_scores_kernel(
                     start=True,
                     stop=True,
                 )
-            d_sb = ring.tile([P, BANK], F32, name="d_sb")
+            d_sb = ring.tile([P, BANK], F32, name="d_sb", bufs=3)
             nc.scalar.copy(d_sb[:], d_ps[:])
-            tanh_d = ring.tile([P, BANK], F32, name="tanh_d")
+            tanh_d = ring.tile([P, BANK], F32, name="tanh_d", bufs=3)
             nc.scalar.activation(tanh_d[:], d_ps[:], ACT.Tanh)
-            top = ring.tile([P, BANK], F32, name="top")
+            top = ring.tile([P, BANK], F32, name="top", bufs=3)
             nc.vector.tensor_tensor(top[:], e_ps[:], d_sb[:], ALU.max)
+            terms[c] = (tanh_d, top)
+
+        def join(c):
+            j0, jn, m0, mn = CHUNKS[c]
+            blocks = jn // P
+            tanh_d, top = terms[c]
+            y_ps = y_bank[c % 2]
             for u in range(mn // P):
                 for b in range(blocks):
                     src = slice(b * mn + u * P, b * mn + (u + 1) * P)
@@ -271,27 +301,39 @@ def tile_list_promotion_page_scores_kernel(
             j0, jn, m0, mn = CHUNKS[c]
             for u in range(mn // P):
                 mt = m0 // P + u
-                y_sb = ring.tile([P, jn], F32, name="y_sb", bufs=4)
+                piece = sum(CHUNKS[k][3] // P for k in range(c)) + u
+                y_sb = stage[piece % 6][:, 0:jn]
                 nc.scalar.activation(
-                    y_sb[:], y_bank[c % 2][:, u * jn : (u + 1) * jn], ACT.Copy, scale=gs_sb[:, mt : mt + 1]
+                    y_sb, y_bank[c % 2][:, u * jn : (u + 1) * jn], ACT.Copy, scale=gs_sb[:, mt : mt + 1]
                 )
                 nc.vector.tensor_tensor(
                     page[mt][:].indirect(idx3[:, j0 // STRIPE : (j0 + jn) // STRIPE]),
-                    y_sb[:], wgo_sb[:, j0 : j0 + jn], ALU.mult,
+                    y_sb, wgo_sb[:, j0 : j0 + jn], ALU.mult,
                 )
                 if j0 + jn == S:
                     nc.sync.dma_start(out[mt * P : (mt + 1) * P, :], page[mt][:])
 
-        direct_weights(0)
-        styles()
         features(0)
         features(1)
+        direct_weights(0)
+        quantise_features(0)
+        styles()
+        quantise_features(1)
         scores(0)
-        for c in range(1, len(CHUNKS)):
-            if c + 1 < 4:
-                features(c + 1)
-            if c == 3:
-                direct_weights(1)
-            scores(c)
-            place(c - 1)
-        place(len(CHUNKS) - 1)
+        features(2)
+        features(3)
+        scores(1)
+        join(0)
+        join(1)
+        place(0)
+        quantise_features(2)
+        quantise_features(3)
+        scores(2)
+        scores(3)
+        place(1)
+        direct_weights(1)
+        for c in range(2, len(CHUNKS)):
+            if c + 2 < len(CHUNKS):
+                scores(c + 2)
+            join(c)
+            place(c)

@@ -72,7 +72,13 @@ def tile_list_promotion_page_scores_kernel(
         h_s = [held([P, QUARTER], U8, "h_s%d" % q) for q in range(4)]
         wgo_sb = held([P, S], F32, "wgo_sb")
         page = [held([P, T2], F32, "page%d" % mt) for mt in range(S2 // P)]
-        stage = [held([P, BANK], F32, "stage%d" % i) for i in range(6)]
+        stage = [held([P, BANK], F32, "stage%d" % i) for i in range(7)]
+        d_stage = [held([P, BANK], F32, "d_stage%d" % i) for i in range(3)]
+        wd_bf_tiles = [stage[0:3], [stage[0], stage[1], stage[5]]]
+        h_rows_tiles = [stage[3], stage[4], stage[0], stage[1]]
+        h_bf_tiles = [stage[5], stage[6], stage[5], stage[6]]
+        y_tiles = [stage[0], stage[1], stage[5], stage[6], stage[3], stage[4], stage[5], d_stage[1],
+                   stage[2], stage[0], stage[1], stage[6]]
         ident = held([P, P], F32, "ident")
 
         x_bank = [psum.tile([P, BANK], F32, name="x_bank%d" % i) for i in range(2)]
@@ -96,8 +102,8 @@ def tile_list_promotion_page_scores_kernel(
         def load_words(tile, words):
             nc.sync.dma_start(tile, words.rearrange("p n t -> p (n t)").bitcast(I32))
 
-        def load_tab(a, h):
-            cols = slice(h * T // 2, (h + 1) * T // 2)
+        def load_tab(a, first, last):
+            cols = slice(first * T // 4, last * T // 4)
             load_words(tab_w[a][:, cols], tab_words[a, :, cols, :])
 
         def move_scales(a):
@@ -113,8 +119,8 @@ def tile_list_promotion_page_scores_kernel(
                 clock_sb[q][:], clock[:, q * QUARTER : (q + 1) * QUARTER].rearrange("(p t) j -> p t j", t=PACK)
             )
 
-        def load_wd(g, passes):
-            for a in passes:
+        def load_wd(g):
+            for a in range(PASSES):
                 rows = wd[a * K_PASS : (a + 1) * K_PASS, g * M_HALF : (g + 1) * M_HALF]
                 nc.sync.dma_start(wd_raw[a, g][:], rows.rearrange("(p t) m -> p t m", t=PACK))
 
@@ -130,7 +136,7 @@ def tile_list_promotion_page_scores_kernel(
             w1_raw[:].bitcast(I32).rearrange("p (a n) -> p a n", a=PASSES),
             w1_words.bitcast(I32).rearrange("a p n -> p a n"),
         )
-        load_tab(0, 0)
+        load_tab(0, 0, 2)
         for a in range(1, PASSES):
             first = PARKED[a - 1]
             nc.sync.dma_start(tab_s[first : first + 16, :].bitcast(I32), tab_scales[a].bitcast(I32))
@@ -138,26 +144,27 @@ def tile_list_promotion_page_scores_kernel(
             nc.sync.dma_start(
                 tab_s[32 * q : 32 * q + 4, :].bitcast(I32), tab_scales[0, 4 * q : 4 * q + 4, :].bitcast(I32)
             )
-        load_tab(0, 1)
+        load_tab(0, 2, 4)
         for q in range(4):
             nc.sync.dma_start(
                 w1_raw_s[32 * q : 32 * q + 4, :].bitcast(I32).rearrange("r (a n) -> r a n", a=PASSES),
                 w1_scales[:, 4 * q : 4 * q + 4, :].bitcast(I32).rearrange("a r n -> r a n"),
             )
-        load_tab(1, 0)
-        nc.vector.tensor_copy(v_s0[:], tab_s[:].indirect(idx[:]))
-        move_scales(1)
-        load_tab(1, 1)
-        move_scales(2)
-        load_tab(2, 0)
+        load_tab(1, 0, 2)
         nc.sync.dma_start(idx2[:], offs2)
         for q in range(4):
             nc.sync.dma_start(
                 tab2_s[32 * q : 32 * q + 4, :].bitcast(I32), tab2_scales[0, 4 * q : 4 * q + 4, :].bitcast(I32)
             )
-        load_tab(2, 1)
+        load_tab(1, 2, 4)
+        nc.vector.tensor_copy(v_s0[:], tab_s[:].indirect(idx[:]))
+        move_scales(1)
+        load_tab(2, 0, 2)
+        move_scales(2)
+        load_tab(2, 2, 3)
+        load_tab(2, 3, 4)
         nc.sync.dma_start(b1_sb[:], b1.rearrange("(p t) -> p t", t=PACK))
-        load_wd(0, range(PASSES))
+        load_wd(0)
         load_clock(0)
         for h in range(2):
             cols = slice(h * T3 // 2, (h + 1) * T3 // 2)
@@ -168,16 +175,15 @@ def tile_list_promotion_page_scores_kernel(
         nc.sync.dma_start(idx3[:], offs3)
         load_wgo(0)
         load_page(0)
-        load_page(1)
         load_clock(2)
+        load_page(1)
         load_clock(3)
-        load_wd(1, range(0, 1))
         load_wgo(1)
-        load_wd(1, range(1, PASSES))
-        load_page(2)
+        load_wd(1)
         load_wgo(2)
-        load_page(3)
+        load_page(2)
         load_wgo(3)
+        load_page(3)
 
         make_identity(nc, ident[:])
 
@@ -222,23 +228,29 @@ def tile_list_promotion_page_scores_kernel(
 
         def quantise_features(q):
             feat = feats[q]
-            h_bf = stage[(q + 4) % 6][:].bitcast(BF16)
+            h_rows = h_rows_tiles[q][:].bitcast(BF16)
             nc.vector.tensor_tensor(
+                h_rows, feat[:].rearrange("p t j -> p (t j)"), clock_sb[q][:].rearrange("p t j -> p (t j)"), ALU.mult
+            )
+            h_bf = h_bf_tiles[q][:].bitcast(BF16)
+            nc.scalar.copy(
                 h_bf.rearrange("p (c i t) -> p c t i", i=4, t=PACK),
-                feat[:].rearrange("p t (c i) -> p c t i", i=4),
-                clock_sb[q][:].rearrange("p t (c i) -> p c t i", i=4),
-                ALU.mult,
+                h_rows.rearrange("p (t c i) -> p c t i", i=4, t=PACK),
             )
             nc.vector.quantize_mx(
                 out=h_w[q][:].bitcast(FP8X4), scales=h_s[q][:], in_=h_bf
             )
 
         def styles():
-            nc.vector.tensor_copy(v2_w[:], tab2_w[:].bitcast(U32).indirect(idx2[:]))
+            for g in range(2):
+                nc.vector.tensor_copy(
+                    v2_w[:, g * M_HALF : (g + 1) * M_HALF],
+                    tab2_w[:].bitcast(U32).indirect(idx2[:, g * M_HALF // STRIPE : (g + 1) * M_HALF // STRIPE]),
+                )
 
         def direct_weights(g):
             for a in range(PASSES):
-                wd_bf = stage[a][:].bitcast(BF16)
+                wd_bf = wd_bf_tiles[g][a][:].bitcast(BF16)
                 cast = nc.vector.tensor_copy if g == 0 and a < PASSES - 1 else nc.scalar.copy
                 cast(
                     wd_bf.rearrange("p (c i t) -> p c t i", i=4, t=PACK),
@@ -277,7 +289,7 @@ def tile_list_promotion_page_scores_kernel(
                     start=True,
                     stop=True,
                 )
-            d_sb = ring.tile([P, BANK], F32, name="d_sb", bufs=3)
+            d_sb = d_stage[c % 3]
             nc.scalar.copy(d_sb[:], d_ps[:])
             tanh_d = ring.tile([P, BANK], F32, name="tanh_d", bufs=3)
             nc.scalar.activation(tanh_d[:], d_ps[:], ACT.Tanh)
@@ -302,7 +314,7 @@ def tile_list_promotion_page_scores_kernel(
             for u in range(mn // P):
                 mt = m0 // P + u
                 piece = sum(CHUNKS[k][3] // P for k in range(c)) + u
-                y_sb = stage[piece % 6][:, 0:jn]
+                y_sb = y_tiles[piece][:, 0:jn]
                 nc.scalar.activation(
                     y_sb, y_bank[c % 2][:, u * jn : (u + 1) * jn], ACT.Copy, scale=gs_sb[:, mt : mt + 1]
                 )

from contextlib import ExitStack

import concourse.mybir as mybir
from concourse.masks import make_identity

K, T, S, H, S2, T3, T2 = 1536, 4096, 1024, 512, 512, 2048, 2048
FLOPS = 2 * (K * H * S + H * S2 * S + K * S2 * S)

F32 = mybir.dt.float32
BF16 = mybir.dt.bfloat16
I32 = mybir.dt.int32
U32 = mybir.dt.uint32
U16 = mybir.dt.uint16
U8 = mybir.dt.uint8
FP8X4 = mybir.dt.float8_e4m3fn_x4
FP4X4 = mybir.dt.float4_e2m1fn_x4
ACT = mybir.ActivationFunctionType
ALU = mybir.AluOpType

P = 128
PACK = 4
K_PASS = P * PACK
PASSES = K // K_PASS
BANK = 512
QUARTER = S // 4
HALF = S // 2
M_HALF = S2 // 2
STRIPE = 16
PARKED = (4, 68)

CHUNKS = [(q * QUARTER, QUARTER, 0, M_HALF) for q in range(4)] + [
    (h * HALF, HALF, mt * P, P) for mt in (2, 3) for h in range(2)
]


def tile_list_promotion_page_scores_kernel(
    tc, tab_words, tab_scales, offs, tab2_words, tab2_scales, offs2, offs3,
    w1_words, w1_scales, b1, clock, wd, gs, wgo, page1, out,
):
    nc = tc.nc
    with ExitStack() as ctx:
        keep = ctx.enter_context(tc.tile_pool(name="keep", bufs=1))
        ring = ctx.enter_context(tc.tile_pool(name="ring", bufs=2))
        psum = ctx.enter_context(tc.psum_pool(name="psum", bufs=1))

        def held(shape, dtype, name):
            return keep.tile(shape, dtype, name=name, align_bytes=64)

        idx = held([P, S // STRIPE], U16, "idx")
        idx2 = held([P, S2 // STRIPE], U16, "idx2")
        idx3 = held([P, S // STRIPE], U16, "idx3")
        tab_w = [held([P, T], I32, "tab_w%d" % a) for a in range(PASSES)]
        tab_s = held([P, T], U8, "tab_s")
        tab2_w = held([P, T3], I32, "tab2_w")
        tab2_s = held([P, T3], U8, "tab2_s")
        w1_raw = held([P, PASSES * 2 * H], U8, "w1_raw")
        w1_raw_s = held([P, PASSES * H], U8, "w1_raw_s")
        w1_w = held([P, PASSES * 2 * H], U8, "w1_w")
        w1_s = held([P, PASSES * H], U8, "w1_s")
        v_w = [held([P, S], U32, "v_w%d" % a) for a in range(PASSES)]
        v_s0 = held([P, S], U8, "v_s0")
        v_s12 = held([P, (PASSES - 1) * S], U8, "v_s12")
        v2_w = held([P, S2], U32, "v2_w")
        v2_s = held([P, S2], U8, "v2_s")
        b1_sb = held([P, PACK], F32, "b1_sb")
        gs_sb = held([P, S2 // P], F32, "gs_sb")
        clock_sb = [held([P, PACK, QUARTER], F32, "clock%d" % q) for q in range(4)]
        wd_raw = {(a, g): held([P, PACK, M_HALF], F32, "wd_raw%d%d" % (a, g)) for g in range(2) for a in range(PASSES)}
        wd_w = {(a, g): held([P, M_HALF], U32, "wd_w%d%d" % (a, g)) for g in range(2) for a in range(PASSES)}
        wd_s = {(a, g): held([P, M_HALF], U8, "wd_s%d%d" % (a, g)) for g in range(2) for a in range(PASSES)}
        h_w = [held([P, QUARTER], U32, "h_w%d" % q) for q in range(4)]
        h_s = [held([P, QUARTER], U8, "h_s%d" % q) for q in range(4)]
        wgo_sb = held([P, S], F32, "wgo_sb")
        page = [held([P, T2], F32, "page%d" % mt) for mt in range(S2 // P)]
        stage = [held([P, BANK], F32, "stage%d" % i) for i in range(7)]
        d_stage = [held([P, BANK], F32, "d_stage%d" % i) for i in range(3)]
        wd_bf_tiles = [stage[0:3], [stage[0], stage[1], stage[5]]]
        h_rows_tiles = [stage[3], stage[4], stage[0], stage[1]]
        h_bf_tiles = [stage[5], stage[6], stage[5], stage[6]]
        y_tiles = [stage[0], stage[1], stage[5], stage[6], stage[3], stage[4], stage[5], d_stage[1],
                   stage[2], stage[0], stage[1], stage[6]]
        ident = held([P, P], F32, "ident")

        x_bank = [psum.tile([P, BANK], F32, name="x_bank%d" % i) for i in range(2)]
        e_bank = [psum.tile([P, BANK], F32, name="e_bank%d" % i) for i in range(2)]
        d_bank = [psum.tile([P, BANK], F32, name="d_bank%d" % i) for i in range(2)]
        y_bank = [psum.tile([P, BANK], F32, name="y_bank%d" % i) for i in range(2)]

        score_banks = [(e_bank[0], d_bank[0]), (e_bank[1], d_bank[1]), (x_bank[0], x_bank[1])]
        feature_banks = [x_bank, score_banks[1], y_bank, x_bank]
        terms = {}
        feats = {}

        def v_scales(a, cols):
            if a == 0:
                return v_s0[:, cols]
            return v_s12[:, (a - 1) * S + cols.start : (a - 1) * S + cols.stop]

        for tile in (tab_s, w1_raw_s, v_s12, tab2_s):
            nc.vector.memset(tile[:].bitcast(I32), 0)

        def load_words(tile, words):
            nc.sync.dma_start(tile, words.rearrange("p n t -> p (n t)").bitcast(I32))

        def load_tab(a, first, last):
            cols = slice(first * T // 4, last * T // 4)
            load_words(tab_w[a][:, cols], tab_words[a, :, cols, :])

        def move_scales(a):
            for q in range(4):
                first = PARKED[a - 1] + 4 * q
                nc.sync.dma_start(
                    v_s12[32 * q : 32 * q + 4, (a - 1) * S : a * S].bitcast(I32),
                    v_s0[first : first + 4, :].bitcast(I32),
                )

        def load_clock(q):
            nc.sync.dma_start(
                clock_sb[q][:], clock[:, q * QUARTER : (q + 1) * QUARTER].rearrange("(p t) j -> p t j", t=PACK)
            )

        def load_wd(g):
            for a in range(PASSES):
                rows = wd[a * K_PASS : (a + 1) * K_PASS, g * M_HALF : (g + 1) * M_HALF]
                nc.sync.dma_start(wd_raw[a, g][:], rows.rearrange("(p t) m -> p t m", t=PACK))

        def load_page(mt):
            nc.sync.dma_start(page[mt][:], page1[mt * P : (mt + 1) * P, :])

        def load_wgo(q):
            cols = slice(q * QUARTER, (q + 1) * QUARTER)
            nc.sync.dma_start(wgo_sb[:, cols], wgo[:, cols])

        nc.sync.dma_start(idx[:], offs)
        nc.sync.dma_start(
            w1_raw[:].bitcast(I32).rearrange("p (a n) -> p a n", a=PASSES),
            w1_words.bitcast(I32).rearrange("a p n -> p a n"),
        )
        load_tab(0, 0, 2)
        for a in range(1, PASSES):
            first = PARKED[a - 1]
            nc.sync.dma_start(tab_s[first : first + 16, :].bitcast(I32), tab_scales[a].bitcast(I32))
        for q in range(4):
            nc.sync.dma_start(
                tab_s[32 * q : 32 * q + 4, :].bitcast(I32), tab_scales[0, 4 * q : 4 * q + 4, :].bitcast(I32)
            )
        load_tab(0, 2, 4)
        for q in range(4):
            nc.sync.dma_start(
                w1_raw_s[32 * q : 32 * q + 4, :].bitcast(I32).rearrange("r (a n) -> r a n", a=PASSES),
                w1_scales[:, 4 * q : 4 * q + 4, :].bitcast(I32).rearrange("a r n -> r a n"),
            )
        load_tab(1, 0, 2)
        nc.sync.dma_start(idx2[:], offs2)
        for q in range(4):
            nc.sync.dma_start(
                tab2_s[32 * q : 32 * q + 4, :].bitcast(I32), tab2_scales[0, 4 * q : 4 * q + 4, :].bitcast(I32)
            )
        load_tab(1, 2, 4)
        nc.vector.tensor_copy(v_s0[:], tab_s[:].indirect(idx[:]))
        move_scales(1)
        load_tab(2, 0, 2)
        move_scales(2)
        load_tab(2, 2, 3)
        load_tab(2, 3, 4)
        nc.sync.dma_start(b1_sb[:], b1.rearrange("(p t) -> p t", t=PACK))
        load_wd(0)
        load_clock(0)
        for h in range(2):
            cols = slice(h * T3 // 2, (h + 1) * T3 // 2)
            load_words(tab2_w[:, cols], tab2_words[0, :, cols, :])
        load_clock(1)
        with nc.allow_non_contiguous_dma(reason="one gain for each partition"):
            nc.sync.dma_start(gs_sb[:], gs.rearrange("(mt p) -> p mt", p=P))
        nc.sync.dma_start(idx3[:], offs3)
        load_wgo(0)
        load_page(0)
        load_clock(2)
        load_page(1)
        load_clock(3)
        load_wgo(1)
        load_wd(1)
        load_wgo(2)
        load_page(2)
        load_wgo(3)
        load_page(3)

        make_identity(nc, ident[:])

        nc.vector.tensor_copy(
            w1_w[:].bitcast(U16).rearrange("p (a t c i) -> p a c t i", a=PASSES, t=PACK, i=8),
            w1_raw[:].bitcast(U16).rearrange("p (a c i t) -> p a c t i", a=PASSES, t=PACK, i=8),
        )
        nc.vector.tensor_copy(
            w1_s[:].rearrange("p (a t c i) -> p a c t i", a=PASSES, t=PACK, i=16),
            w1_raw_s[:].rearrange("p (a c i t) -> p a c t i", a=PASSES, t=PACK, i=16),
        )
        for a in range(PASSES - 1):
            nc.vector.tensor_copy(v_w[a][:], tab_w[a][:].bitcast(U32).indirect(idx[:]))
        nc.vector.tensor_copy(v2_s[:], tab2_s[:].indirect(idx2[:]))
        for h in range(2):
            nc.vector.tensor_copy(
                v_w[PASSES - 1][:, h * HALF : (h + 1) * HALF],
                tab_w[PASSES - 1][:].bitcast(U32).indirect(idx[:, h * HALF // STRIPE : (h + 1) * HALF // STRIPE]),
            )

        def features(q):
            cols = slice(q * QUARTER, (q + 1) * QUARTER)
            for a in range(PASSES):
                for t in range(PACK):
                    c0 = a * H + t * P
                    nc.tensor.matmul_mx(
                        out=feature_banks[q][t // 2][:, (t % 2) * QUARTER : (t % 2 + 1) * QUARTER],
                        lhsT=w1_w[:, 2 * c0 : 2 * (c0 + P)].bitcast(FP4X4),
                        lhsT_scale=w1_s[:, c0 : c0 + P],
                        rhs=v_w[a][:, cols].bitcast(FP8X4),
                        rhs_scale=v_scales(a, cols),
                        start=(a == 0 and t % 2 == 0),
                        stop=(a == PASSES - 1 and t % 2 == 1),
                    )
            feat = ring.tile([P, PACK, QUARTER], F32, name="feat", bufs=4)
            for t in range(PACK):
                nc.scalar.activation(
                    feat[:, t, :], feature_banks[q][t // 2][:, (t % 2) * QUARTER : (t % 2 + 1) * QUARTER],
                    ACT.Tanh, bias=b1_sb[:, t : t + 1],
                )
            feats[q] = feat

        def quantise_features(q):
            feat = feats[q]
            h_rows = h_rows_tiles[q][:].bitcast(BF16)
            nc.vector.tensor_tensor(
                h_rows, feat[:].rearrange("p t j -> p (t j)"), clock_sb[q][:].rearrange("p t j -> p (t j)"), ALU.mult
            )
            h_bf = h_bf_tiles[q][:].bitcast(BF16)
            nc.scalar.copy(
                h_bf.rearrange("p (c i t) -> p c t i", i=4, t=PACK),
                h_rows.rearrange("p (t c i) -> p c t i", i=4, t=PACK),
            )
            nc.vector.quantize_mx(
                out=h_w[q][:].bitcast(FP8X4), scales=h_s[q][:], in_=h_bf
            )

        def styles():
            for g in range(2):
                nc.vector.tensor_copy(
                    v2_w[:, g * M_HALF : (g + 1) * M_HALF],
                    tab2_w[:].bitcast(U32).indirect(idx2[:, g * M_HALF // STRIPE : (g + 1) * M_HALF // STRIPE]),
                )

        def direct_weights(g):
            for a in range(PASSES):
                wd_bf = wd_bf_tiles[g][a][:].bitcast(BF16)
                cast = nc.vector.tensor_copy if g == 0 and a < PASSES - 1 else nc.scalar.copy
                cast(
                    wd_bf.rearrange("p (c i t) -> p c t i", i=4, t=PACK),
                    wd_raw[a, g][:].rearrange("p t (c i) -> p c t i", i=4),
                )
                nc.vector.quantize_mx(
                    out=wd_w[a, g][:].bitcast(FP8X4), scales=wd_s[a, g][:],
                    in_=wd_bf,
                )

        def scores(c):
            j0, jn, m0, mn = CHUNKS[c]
            blocks = jn // P
            g, mc = divmod(m0, M_HALF)
            e_ps, d_ps = score_banks[c % 3]
            for a in range(PASSES):
                for b in range(blocks):
                    cols = slice(j0 + b * P, j0 + (b + 1) * P)
                    nc.tensor.matmul_mx(
                        out=d_ps[:, b * mn : (b + 1) * mn],
                        lhsT=v_w[a][:, cols].bitcast(FP8X4),
                        lhsT_scale=v_scales(a, cols),
                        rhs=wd_w[a, g][:, mc : mc + mn].bitcast(FP8X4),
                        rhs_scale=wd_s[a, g][:, mc : mc + mn],
                        start=(a == 0 and b == 0),
                        stop=(a == PASSES - 1 and b == blocks - 1),
                    )
            for b in range(blocks):
                q, jc = divmod(j0 + b * P, QUARTER)
                nc.tensor.matmul_mx(
                    out=e_ps[:, b * mn : (b + 1) * mn],
                    lhsT=h_w[q][:, jc : jc + P].bitcast(FP8X4),
                    lhsT_scale=h_s[q][:, jc : jc + P],
                    rhs=v2_w[:, m0 : m0 + mn].bitcast(FP8X4),
                    rhs_scale=v2_s[:, m0 : m0 + mn],
                    start=True,
                    stop=True,
                )
            d_sb = d_stage[c % 3]
            nc.scalar.copy(d_sb[:], d_ps[:])
            tanh_d = ring.tile([P, BANK], F32, name="tanh_d", bufs=3)
            nc.scalar.activation(tanh_d[:], d_ps[:], ACT.Tanh)
            top = ring.tile([P, BANK], F32, name="top", bufs=3)
            nc.vector.tensor_tensor(top[:], e_ps[:], d_sb[:], ALU.max)
            terms[c] = (tanh_d, top)

        def join(c):
            j0, jn, m0, mn = CHUNKS[c]
            blocks = jn // P
            tanh_d, top = terms[c]
            y_ps = y_bank[c % 2]
            for u in range(mn // P):
                for b in range(blocks):
                    src = slice(b * mn + u * P, b * mn + (u + 1) * P)
                    dst = y_ps[:, u * jn + b * P : u * jn + (b + 1) * P]
                    nc.tensor.matmul(dst, tanh_d[:, src], ident[:], start=True, stop=False, is_transpose=True)
                    nc.tensor.matmul(dst, top[:, src], ident[:], start=False, stop=True, is_transpose=True)

        def place(c):
            j0, jn, m0, mn = CHUNKS[c]
            for u in range(mn // P):
                mt = m0 // P + u
                piece = sum(CHUNKS[k][3] // P for k in range(c)) + u
                y_sb = y_tiles[piece][:, 0:jn]
                nc.scalar.activation(
                    y_sb, y_bank[c % 2][:, u * jn : (u + 1) * jn], ACT.Copy, scale=gs_sb[:, mt : mt + 1]
                )
                nc.vector.tensor_tensor(
                    page[mt][:].indirect(idx3[:, j0 // STRIPE : (j0 + jn) // STRIPE]),
                    y_sb, wgo_sb[:, j0 : j0 + jn], ALU.mult,
                )
                if j0 + jn == S:
                    nc.sync.dma_start(out[mt * P : (mt + 1) * P, :], page[mt][:])

        features(0)
        features(1)
        direct_weights(0)
        quantise_features(0)
        styles()
        quantise_features(1)
        scores(0)
        features(2)
        features(3)
        scores(1)
        join(0)
        join(1)
        place(0)
        quantise_features(2)
        quantise_features(3)
        scores(2)
        scores(3)
        place(1)
        direct_weights(1)
        for c in range(2, len(CHUNKS)):
            if c + 2 < len(CHUNKS):
                scores(c + 2)
            join(c)
            place(c)
